import numpy as np
import ml_dtypes


def mxq(x, axis, fmt="e4m3"):
    dtype, down = {"e4m3": (ml_dtypes.float8_e4m3fn, 7), "e5m2": (ml_dtypes.float8_e5m2, 14)}[fmt]
    v = np.moveaxis(np.asarray(x, np.float32).astype(ml_dtypes.bfloat16).astype(np.float64), axis, -1)
    blocks = v.reshape(v.shape[:-1] + (-1, 32))
    amax = np.abs(blocks).max(-1, keepdims=True)
    byte = np.maximum(np.where(amax > 0, np.frexp(amax)[1] - 1 + 127, 0) - down, 1)
    scale = np.exp2(byte - 127.0)
    codes = (blocks / scale).astype(np.float32).astype(dtype).astype(np.float64)
    return np.moveaxis((codes * scale).reshape(v.shape), -1, axis)


WIDE = False


def mx_kscale(k):
    if not WIDE:
        return np.ones(k)
    levels = np.array([10, -10, 5, -5, 0])
    if k % 512:
        return np.exp2(np.random.permutation(np.resize(levels, k // 32))).repeat(32)
    a = np.empty((k // 512, 16))
    for p in range(k // 512):
        a[p, :8] = np.random.permutation(np.resize(levels, 8))
        for g in range(8):
            far = levels[np.abs(levels - a[p, g]) >= 10]
            a[p, g + 8] = far[np.random.randint(len(far))]
    return np.exp2(a.ravel()).repeat(32)


def f64(x):
    return np.asarray(x).astype(np.float64)


def striped(idx):
    return np.tile(idx.reshape(-1, 16).T, (8, 1)).astype(np.uint16)


def unstriped(offs):
    return offs[:16].T.reshape(-1).astype(np.int64)


E2M1 = np.array([0.0, 0.5, 1.0, 1.5, 2.0, 3.0, 4.0, 6.0, -0.0, -0.5, -1.0, -1.5, -2.0, -3.0, -4.0, -6.0])


def pack_weight(w, fmt):
    k, n = w.shape
    w = f64(np.asarray(w, np.float32).astype(ml_dtypes.bfloat16)).reshape(k // 32, 32, n)
    amax = np.abs(w).max(1)
    if fmt == "e4m3":
        byte = np.frexp(amax)[1] - 1 + 127 - 7
    else:
        mant, ex = np.frexp(amax / 6.0)
        byte = np.where(mant > 0.5, ex, ex - 1) + 127
    byte = np.clip(np.where(amax > 0, byte, 1), 1, 254)
    scaled = (w * np.exp2(127.0 - byte)[:, None, :]).reshape(k, n).astype(np.float32)
    by_word = np.ascontiguousarray(scaled.reshape(k // 512, 128, 4, n).transpose(0, 1, 3, 2))
    if fmt == "e4m3":
        words = by_word.astype(ml_dtypes.float8_e4m3fn).view(np.uint8)
    else:
        c = by_word.astype(ml_dtypes.float4_e2m1fn).view(np.uint8) & 0xF
        words = (c[..., 0::2] | (c[..., 1::2] << 4)).reshape(k // 512, 128, 2 * n)
    return np.ascontiguousarray(words), np.ascontiguousarray(byte.astype(np.uint8).reshape(k // 512, 16, n))


def unpack_weight(words, scales, fmt):
    g, _, n = scales.shape
    words = np.ascontiguousarray(words).reshape(g, 128, n, -1)
    if fmt == "e4m3":
        vals = words.view(ml_dtypes.float8_e4m3fn).astype(np.float64)
    else:
        nib = np.empty((g, 128, n, 4), np.uint8)
        nib[..., 0::2] = words & 0xF
        nib[..., 1::2] = words >> 4
        vals = E2M1[nib]
    vals = vals * np.repeat(np.exp2(scales.astype(np.float64) - 127.0), 8, axis=1)[..., None]
    return vals.transpose(0, 1, 3, 2).reshape(g * 512, n)


def gelu(v):
    return 0.5 * v * (1.0 + np.tanh(np.sqrt(2.0 / np.pi) * (v + 0.044715 * v**3)))


K, T, H, S, T2, T3, S2, P = 1024, 2048, 1024, 512, 1024, 2048, 512, 512

def setup_inputs():
    n = np.random.standard_normal
    s = mx_kscale(K)[:, None]
    u = mx_kscale(H)[:, None]
    tab_words, tab_scales = pack_weight(n((K, T)) * s, "e4m3")
    tab2_words, tab2_scales = pack_weight(n((H, T3)) / np.sqrt(H) / u, "e4m3")
    w2_words, w2_scales = pack_weight(n((K, H)) / np.sqrt(K) / s * u.T, "e2m1")
    w3_words, w3_scales = pack_weight(n((K, H)) / np.sqrt(K) / s * u.T, "e4m3")
    return {
        "tab_words": tab_words, "tab_scales": tab_scales,
        "tab2_words": tab2_words, "tab2_scales": tab2_scales,
        "w1": (n((K, H)) / np.sqrt(K) / s * u.T).astype(np.float32),
        "w2_words": w2_words, "w2_scales": w2_scales,
        "w3_words": w3_words, "w3_scales": w3_scales,
        "page0": (n((H, T2)) * u).astype(np.float32),
        "wgs": np.exp(0.3 * n((128, S))).astype(np.float32),
        "see": np.exp(0.3 * n(T2)).astype(np.float32),
        "path": n(S2).astype(np.float32),
        "base": n((S2, P)).astype(np.float32),
        "offs": striped(np.random.permutation(T)[:S]),
        "offs2": striped(np.random.permutation(T3)[:S2]),
        "offs3": striped(np.random.permutation(T2)[:S]),
        "pos1": striped(np.random.permutation(T2)[:P]),
        "pos2": striped(np.random.permutation(T2)[:P]),
    }

def reference(tab_words, tab_scales, tab2_words, tab2_scales, w1, w2_words, w2_scales, w3_words, w3_scales,
              page0, wgs, see, path, base, offs, offs2, offs3, pos1, pos2):
    v = unpack_weight(tab_words, tab_scales, "e4m3")[:, unstriped(offs)]
    v2 = unpack_weight(tab2_words, tab2_scales, "e4m3")[:, unstriped(offs2)]
    d1 = mxq(f64(w1), 0, "e4m3").T @ v
    d2 = unpack_weight(w2_words, w2_scales, "e2m1").T @ v
    d3 = unpack_weight(w3_words, w3_scales, "e4m3").T @ v
    h = np.maximum(np.maximum(d1, d2), d3)
    page = f64(page0).copy()
    page[:, unstriped(offs3)] = np.tile(f64(wgs), (H // 128, 1)) * h
    seen = page * f64(see)[None, :]
    e = v2.T @ mxq(seen, 0, "e4m3")
    first = e[:, unstriped(pos1)] + f64(path)[:, None]
    second = np.maximum(e[:, unstriped(pos2)], f64(base))
    return first * second

@@ -1,0 +1,318 @@
+from contextlib import ExitStack
+
+import concourse.mybir as mybir
+from concourse.masks import make_identity
+
+K, T, H, S, T2, S2 = 1024, 2048, 1024, 512, 1024, 512
+FLOPS = 3 * 2 * K * H * S + 2 * H * S2 * T2
+
+F32 = mybir.dt.float32
+BF16 = mybir.dt.bfloat16
+I32 = mybir.dt.int32
+U32 = mybir.dt.uint32
+U16 = mybir.dt.uint16
+U8 = mybir.dt.uint8
+FP8X4 = mybir.dt.float8_e4m3fn_x4
+FP4X4 = mybir.dt.float4_e2m1fn_x4
+MULT = mybir.AluOpType.mult
+ADD = mybir.AluOpType.add
+MAX = mybir.AluOpType.max
+COPY = mybir.ActivationFunctionType.Copy
+
+P = 128
+PASSES = 2
+BANK = 512
+SLICES = H // P
+N_TILES = T2 // P
+M_TILES = S2 // P
+W1_CHUNKS = ((0, 1), (1, 2), (2, 4), (4, 6), (6, 8))
+WQ_CHUNKS = ((0, 1), (1, 4), (4, 8))
+
+
+def tile_list_comet_page_triage_kernel(
+    tc, tab_words, tab_scales, tab2_words, tab2_scales, w1, w2_words, w2_scales, w3_words, w3_scales,
+    page0, wgs, see, path, base, offs, offs2, offs3, pos1, pos2, out,
+):
+    nc = tc.nc
+    with ExitStack() as ctx:
+        keep = ctx.enter_context(tc.tile_pool(name="keep", bufs=1))
+        ring2 = ctx.enter_context(tc.tile_pool(name="ring2", bufs=2))
+        ring3 = ctx.enter_context(tc.tile_pool(name="ring3", bufs=3))
+        psum_mx = ctx.enter_context(tc.psum_pool(name="psum_mx", bufs=4))
+        psum_t = ctx.enter_context(tc.psum_pool(name="psum_t", bufs=2))
+
+        def load_list(name, src):
+            t = keep.tile([P, S // 16], U16, name=name)
+            nc.sync.dma_start(t[:], src)
+            return t
+
+        def load_table_words(name, words, a):
+            t = keep.tile([P, T], U32, name=name)
+            nc.sync.dma_start(t[:].bitcast(I32), words[a].rearrange("p t i -> p (t i)").bitcast(I32))
+            return t
+
+        def load_scales_side_by_side(queue, t, scales):
+            for q in range(4):
+                queue.dma_start(
+                    t[32 * q : 32 * q + 4].bitcast(I32),
+                    scales[:, 4 * q : 4 * q + 4, :].rearrange("a r c -> r a c").bitcast(I32),
+                )
+
+        def load_scales_stacked(queue, t, scales):
+            for q in range(4):
+                queue.dma_start(t[32 * q : 32 * q + 8].bitcast(I32), scales[:, 4 * q : 4 * q + 4, :].bitcast(I32))
+
+        w1_raw, w2_sb, w3_sb, page = {}, {}, {}, {}
+
+        def load_w1(s0, s1):
+            t = keep.tile([P, PASSES, 4, (s1 - s0) * P], F32, name="w1_raw%d" % s0)
+            for a in range(PASSES):
+                rows = w1[BANK * a : BANK * (a + 1), s0 * P : s1 * P]
+                nc.sync.dma_start(t[:, a], rows.rearrange("(p j) c -> p j c", j=4))
+            for s in range(s0, s1):
+                w1_raw[s] = t[:, :, :, (s - s0) * P : (s - s0 + 1) * P]
+
+        def load_wq(s0, s1):
+            t3 = keep.tile([P, PASSES, (s1 - s0) * P], U32, name="w3_sb%d" % s0, align_bytes=64)
+            src3 = w3_words.rearrange("a p c i -> p a (c i)")[:, :, 4 * P * s0 : 4 * P * s1]
+            nc.sync.dma_start(t3[:].bitcast(I32), src3.bitcast(I32))
+            t2 = keep.tile([P, PASSES, (s1 - s0) * 2 * P], U8, name="w2_sb%d" % s0, align_bytes=64)
+            src2 = w2_words.rearrange("a p b -> p a b")[:, :, 2 * P * s0 : 2 * P * s1]
+            nc.sync.dma_start(t2[:].bitcast(I32), src2.bitcast(I32))
+            for s in range(s0, s1):
+                w3_sb[s] = t3[:, :, (s - s0) * P : (s - s0 + 1) * P]
+                w2_sb[s] = t2[:, :, (s - s0) * 2 * P : (s - s0 + 1) * 2 * P]
+
+        def load_page(s):
+            page[s] = keep.tile([P, T2], F32, name="page%d" % s)
+            nc.sync.dma_start(page[s][:], page0[s * P : (s + 1) * P, :])
+
+        tab_sc = keep.tile([P, PASSES, T], U8)
+        w3_sc = keep.tile([P, H], U8, align_bytes=64)
+        w2_sc = keep.tile([P, PASSES, H], U8, align_bytes=64)
+        tab2_sc = keep.tile([P, T], U8)
+        nc.vector.memset(tab_sc[:].bitcast(I32), 0)
+        nc.vector.memset(w2_sc[:].bitcast(I32), 0)
+        nc.vector.memset(w3_sc[:].bitcast(I32), 0)
+        nc.gpsimd.memset(tab2_sc[:].bitcast(I32), 0)
+        vec_rows = keep.tile([P, P], F32)
+        nc.gpsimd.memset(vec_rows[:], 0.0)
+        ident = keep.tile([P, P], F32)
+        make_identity(nc, ident[:])
+
+        offs_sb = load_list("offs_sb", offs)
+        tab_w = [load_table_words("tab_w0", tab_words, 0)]
+        load_scales_side_by_side(nc.sync, tab_sc, tab_scales)
+        tab_w.append(load_table_words("tab_w1", tab_words, 1))
+        load_scales_side_by_side(nc.gpsimd, w2_sc, w2_scales)
+        load_w1(*W1_CHUNKS[0])
+        load_wq(*WQ_CHUNKS[0])
+        load_scales_stacked(nc.sync, w3_sc, w3_scales)
+        wgs_sb = keep.tile([P, S], F32)
+        nc.sync.dma_start(wgs_sb[:], wgs)
+        offs3_sb = load_list("offs3_sb", offs3)
+        load_page(0)
+        load_w1(*W1_CHUNKS[1])
+        load_wq(*WQ_CHUNKS[1])
+        load_page(1)
+        nc.sync.dma_start(vec_rows[0:N_TILES, :], see.rearrange("(t p) -> t p", p=P))
+        nc.sync.dma_start(vec_rows[N_TILES : N_TILES + M_TILES, :], path.rearrange("(t p) -> t p", p=P))
+        load_w1(*W1_CHUNKS[2])
+        load_page(2)
+        load_w1(*W1_CHUNKS[3])
+        load_wq(*WQ_CHUNKS[2])
+        load_page(3)
+        load_w1(*W1_CHUNKS[4])
+        for s in range(4, SLICES):
+            load_page(s)
+        offs2_sb = load_list("offs2_sb", offs2)
+        load_scales_stacked(nc.sync, tab2_sc, tab2_scales)
+        tab2_w = [load_table_words("tab2_w%d" % a, tab2_words, a) for a in range(PASSES)]
+        pos1_sb = load_list("pos1_sb", pos1)
+        pos2_sb = load_list("pos2_sb", pos2)
+        base_sb = keep.tile([P, M_TILES, S], F32)
+        nc.sync.dma_start(base_sb[:], base.rearrange("(t p) j -> p t j", p=P))
+
+        v_sc, v_w = [], []
+        for a in range(PASSES):
+            g = keep.tile([P, S], U8, name="v_sc%d" % a, tag="picked_sc%d" % a, align_bytes=64)
+            nc.vector.tensor_copy(g[:], tab_sc[:, a, :].indirect(offs_sb[:]))
+            v_sc.append(g)
+        for a in range(PASSES):
+            g = keep.tile([P, S], U32, name="v_w%d" % a, tag="picked_w%d" % a, align_bytes=64)
+            nc.vector.tensor_copy(g[:], tab_w[a][:].indirect(offs_sb[:]))
+            v_w.append(g)
+
+        w1_q = {}
+        vec_cols = keep.tile([P, N_TILES + M_TILES], F32)
+
+        def turn_vectors():
+            vec_ps = psum_t.tile([P, BANK], F32, tag="back")
+            nc.tensor.transpose(vec_ps[:, 0:P], vec_rows[:], ident[:])
+            nc.scalar.copy(vec_cols[:], vec_ps[:, 0 : N_TILES + M_TILES])
+
+        def quantise_w1(s):
+            grouped = ring3.tile([P, PASSES, P, 4], BF16, align_bytes=64)
+            dst = grouped[:].rearrange("p a (c i) j -> p a c j i", i=4)
+            src = w1_raw[s].rearrange("p a j (c i) -> p a c j i", i=4)
+            if s == 0:
+                nc.vector.tensor_copy(dst, src)
+            else:
+                nc.scalar.copy(dst, src)
+            codes = ring3.tile([P, PASSES * P], U32, align_bytes=64)
+            if s == SLICES - 1:
+                scales = keep.tile([P, PASSES * P], U8, tag="late_scales", align_bytes=64)
+            else:
+                scales = ring3.tile([P, PASSES * P], U8, align_bytes=64)
+            nc.vector.quantize_mx(
+                out=codes[:].bitcast(FP8X4), scales=scales[:], in_=grouped[:].rearrange("p a c j -> p (a c j)")
+            )
+            w1_q[s] = (codes, scales)
+
+        def product(lhs_codes, lhs_scales, rhs_codes, rhs_scales):
+            acc = psum_mx.tile([P, BANK], F32, name="acc")
+            for a in range(PASSES):
+                nc.tensor.matmul_mx(
+                    out=acc[:], lhsT=lhs_codes[a], lhsT_scale=lhs_scales[a],
+                    rhs=rhs_codes[a][:].bitcast(FP8X4), rhs_scale=rhs_scales[a][:],
+                    start=(a == 0), stop=(a == PASSES - 1),
+                )
+            return acc
+
+        def write_slice(s):
+            cols = slice(s * P, (s + 1) * P)
+            d3 = product(
+                [w3_sb[s][:, a, :].bitcast(FP8X4) for a in range(PASSES)],
+                [w3_sc[4 * a : P, cols] for a in range(PASSES)], v_w, v_sc,
+            )
+            d3_sb = ring2.tile([P, S], F32)
+            nc.scalar.copy(d3_sb[:], d3[:])
+            d2 = product(
+                [w2_sb[s][:, a, :].bitcast(FP4X4) for a in range(PASSES)],
+                [w2_sc[:, a, cols] for a in range(PASSES)], v_w, v_sc,
+            )
+            codes, scales = w1_q[s]
+            d1 = product(
+                [codes[:, a * P : (a + 1) * P].bitcast(FP8X4) for a in range(PASSES)],
+                [scales[:, a * P : (a + 1) * P] for a in range(PASSES)], v_w, v_sc,
+            )
+            h = ring2.tile([P, S], F32)
+            nc.vector.tensor_tensor(h[:], d2[:], d3_sb[:], MAX)
+            nc.vector.tensor_tensor(h[:], d1[:], h[:], MAX)
+            nc.vector.tensor_tensor(page[s][:].indirect(offs3_sb[:]), h[:], wgs_sb[:], MULT)
+
+        def weigh(b_t, nt, bank_cols, p0, p1):
+            nc.scalar.activation(
+                b_t[:, :, p0:p1, :], bank_cols.rearrange("n (p u e) -> n u p e", u=2, e=2), COPY,
+                scale=vec_cols[:, nt : nt + 1],
+            )
+
+        def turn_and_weigh(b_t, nt, s0, s1):
+            bank = psum_t.tile([P, BANK], F32, tag="turn")
+            for s in range(s0, s1):
+                nc.tensor.transpose(
+                    bank[:, (s - s0) * P : (s - s0 + 1) * P], page[s][:, nt * P : (nt + 1) * P], ident[:]
+                )
+            weigh(b_t, nt, bank[:, 0 : (s1 - s0) * P], 32 * (s0 % 4), 32 * (s0 % 4) + 32 * (s1 - s0))
+
+        def turn_back(b_pair, woven, j):
+            bank = psum_t.tile([P, 2, 2, P], F32, tag="back")
+            for i in range(2):
+                words = b_pair[i][:].rearrange("n u p e -> n (u p e)").bitcast(F32)
+                for u in range(2):
+                    nc.tensor.transpose(bank[:, i, u, :], words[:, u * P : (u + 1) * P], ident[:])
+            dst = woven.bitcast(F32).rearrange("p (i n u) -> p i n u", i=4, u=2)[:, 2 * j : 2 * j + 2]
+            nc.scalar.copy(dst, bank[:].rearrange("p i u n -> p i n u"))
+
+        b_codes = {}
+        b_scales = {}
+
+        def quantise_b(woven, a, half):
+            b_codes[a, half] = keep.tile([P, BANK], U32, name="b_codes%d%d" % (a, half), align_bytes=64)
+            b_scales[a, half] = keep.tile([P, BANK], U8, name="b_scales%d%d" % (a, half), align_bytes=64)
+            nc.vector.quantize_mx(out=b_codes[a, half][:].bitcast(FP8X4), scales=b_scales[a, half][:], in_=woven[:])
+
+        woven0 = keep.tile([P, 2, 4 * BANK], BF16, align_bytes=64)
+
+        def first_pass_pair(pair):
+            half, j = divmod(pair, 2)
+            b_pair = []
+            for i in range(2):
+                b_t = ring3.tile([P, 2, P, 2], BF16, name="b_t0")
+                turn_and_weigh(b_t, 2 * pair + i, 0, 4)
+                b_pair.append(b_t)
+            turn_back(b_pair, woven0[:, half, :], j)
+
+        b_t1 = [keep.tile([P, 2, P, 2], BF16, name="b_t1_%d" % nt) for nt in range(N_TILES)]
+
+        def turn_one_slice(s):
+            for half in range(2):
+                bank = psum_t.tile([P, BANK], F32, tag="turn")
+                for i in range(4):
+                    nt = 4 * half + i
+                    nc.tensor.transpose(bank[:, i * P : (i + 1) * P], page[s][:, nt * P : (nt + 1) * P], ident[:])
+                for i in range(4):
+                    p0 = 32 * (s % 4)
+                    weigh(b_t1[4 * half + i], 4 * half + i, bank[:, i * P : (i + 1) * P], p0, p0 + 32)
+
+        quantise_w1(0)
+        quantise_w1(1)
+        for s in range(SLICES):
+            write_slice(s)
+            if s + 2 < SLICES:
+                quantise_w1(s + 2)
+            if s == 1:
+                turn_vectors()
+            if s in (4, 5):
+                first_pass_pair(2 * (s - 4))
+                first_pass_pair(2 * (s - 4) + 1)
+            if s == 6:
+                for nt in range(N_TILES):
+                    turn_and_weigh(b_t1[nt], nt, 4, 6)
+        turn_one_slice(6)
+
+        v2_sc = keep.tile([P, S2], U8, tag="picked_sc0", align_bytes=64)
+        nc.vector.tensor_copy(v2_sc[:], tab2_sc[:].indirect(offs2_sb[:]))
+        v2_w = []
+        for a in range(PASSES):
+            g = keep.tile([P, S2], U32, name="v2_w%d" % a, tag="picked_w%d" % a, align_bytes=64)
+            nc.vector.tensor_copy(g[:], tab2_w[a][:].indirect(offs2_sb[:]))
+            v2_w.append(g)
+
+        codes0 = keep.tile([P, T2], U32, align_bytes=64)
+        scales0 = keep.tile([P, T2], U8, tag="late_scales", align_bytes=64)
+        nc.vector.quantize_mx(
+            out=codes0[:].bitcast(FP8X4), scales=scales0[:], in_=woven0[:].rearrange("p h c -> p (h c)")
+        )
+        for half in range(2):
+            b_codes[0, half] = codes0[:, half * BANK : (half + 1) * BANK]
+            b_scales[0, half] = scales0[:, half * BANK : (half + 1) * BANK]
+
+        turn_one_slice(7)
+        for half in range(2):
+            woven = ring2.tile([P, 4 * BANK], BF16, name="woven", align_bytes=64)
+            for j in range(2):
+                turn_back(b_t1[4 * half + 2 * j : 4 * half + 2 * j + 2], woven[:], j)
+            quantise_b(woven, 1, half)
+
+        for m in range(M_TILES):
+            cols = slice(m * P, (m + 1) * P)
+            e = ring3.tile([P, T2], F32)
+            for half in range(2):
+                acc = product(
+                    [v2_w[a][:, cols].bitcast(FP8X4) for a in range(PASSES)],
+                    [v2_sc[4 * a : P, cols] for a in range(PASSES)],
+                    [b_codes[a, half] for a in range(PASSES)],
+                    [b_scales[a, half] for a in range(PASSES)],
+                )
+                nc.scalar.copy(e[:, half * BANK : (half + 1) * BANK], acc[:])
+            second = ring2.tile([P, S], F32)
+            nc.vector.tensor_copy(second[:], e[:].indirect(pos2_sb[:]))
+            first = ring2.tile([P, S], F32)
+            nc.vector.tensor_copy(first[:], e[:].indirect(pos1_sb[:]))
+            nc.vector.tensor_tensor(second[:], second[:], base_sb[:, m, :], MAX)
+            res = ring2.tile([P, S], F32)
+            nc.vector.scalar_tensor_tensor(
+                res[:], first[:], vec_cols[:, N_TILES + m : N_TILES + m + 1], second[:], ADD, MULT
+            )
+            nc.sync.dma_start(out[cols, :], res[:])

@@ -26,7 +26,7 @@ SLICES = H // P
 N_TILES = T2 // P
 M_TILES = S2 // P
 W1_CHUNKS = ((0, 1), (1, 2), (2, 4), (4, 6), (6, 8))
-WQ_CHUNKS = ((0, 1), (1, 4), (4, 8))
+WQ_CHUNKS = ((0, 2), (2, 5), (5, 8))
 
 
 def tile_list_comet_page_triage_kernel(
@@ -103,26 +103,26 @@ def tile_list_comet_page_triage_kernel(
         offs_sb = load_list("offs_sb", offs)
         tab_w = [load_table_words("tab_w0", tab_words, 0)]
         load_scales_side_by_side(nc.sync, tab_sc, tab_scales)
+        load_wq(*WQ_CHUNKS[0])
         tab_w.append(load_table_words("tab_w1", tab_words, 1))
         load_scales_side_by_side(nc.gpsimd, w2_sc, w2_scales)
-        load_w1(*W1_CHUNKS[0])
-        load_wq(*WQ_CHUNKS[0])
         load_scales_stacked(nc.sync, w3_sc, w3_scales)
-        wgs_sb = keep.tile([P, S], F32)
+        load_w1(*W1_CHUNKS[0])
+        wgs_sb = keep.tile([P, S], F32, tag="wgs_then_v2", align_bytes=64)
         nc.sync.dma_start(wgs_sb[:], wgs)
-        offs3_sb = load_list("offs3_sb", offs3)
-        load_page(0)
         load_w1(*W1_CHUNKS[1])
+        load_page(0)
+        offs3_sb = load_list("offs3_sb", offs3)
+        load_w1(*W1_CHUNKS[2])
         load_wq(*WQ_CHUNKS[1])
         load_page(1)
+        load_w1(*W1_CHUNKS[3])
+        load_page(2)
         nc.sync.dma_start(vec_rows[0:N_TILES, :], see.rearrange("(t p) -> t p", p=P))
         nc.sync.dma_start(vec_rows[N_TILES : N_TILES + M_TILES, :], path.rearrange("(t p) -> t p", p=P))
-        load_w1(*W1_CHUNKS[2])
-        load_page(2)
-        load_w1(*W1_CHUNKS[3])
-        load_wq(*WQ_CHUNKS[2])
-        load_page(3)
         load_w1(*W1_CHUNKS[4])
+        load_page(3)
+        load_wq(*WQ_CHUNKS[2])
         for s in range(4, SLICES):
             load_page(s)
         offs2_sb = load_list("offs2_sb", offs2)
@@ -135,13 +135,12 @@ def tile_list_comet_page_triage_kernel(
 
         v_sc, v_w = [], []
         for a in range(PASSES):
+            g = keep.tile([P, S], U32, name="v_w%d" % a, align_bytes=64)
+            nc.vector.tensor_copy(g[:], tab_w[a][:].indirect(offs_sb[:]))
+            v_w.append(g)
             g = keep.tile([P, S], U8, name="v_sc%d" % a, tag="picked_sc%d" % a, align_bytes=64)
             nc.vector.tensor_copy(g[:], tab_sc[:, a, :].indirect(offs_sb[:]))
             v_sc.append(g)
-        for a in range(PASSES):
-            g = keep.tile([P, S], U32, name="v_w%d" % a, tag="picked_w%d" % a, align_bytes=64)
-            nc.vector.tensor_copy(g[:], tab_w[a][:].indirect(offs_sb[:]))
-            v_w.append(g)
 
         w1_q = {}
         vec_cols = keep.tile([P, N_TILES + M_TILES], F32)
@@ -156,14 +155,12 @@ def tile_list_comet_page_triage_kernel(
             dst = grouped[:].rearrange("p a (c i) j -> p a c j i", i=4)
             src = w1_raw[s].rearrange("p a j (c i) -> p a c j i", i=4)
             if s == 0:
-                nc.vector.tensor_copy(dst, src)
+                for a in range(PASSES):
+                    nc.scalar.copy(dst[:, a], src[:, a])
             else:
                 nc.scalar.copy(dst, src)
-            codes = ring3.tile([P, PASSES * P], U32, align_bytes=64)
-            if s == SLICES - 1:
-                scales = keep.tile([P, PASSES * P], U8, tag="late_scales", align_bytes=64)
-            else:
-                scales = ring3.tile([P, PASSES * P], U8, align_bytes=64)
+            codes = keep.tile([P, PASSES * P], U32, name="w1_codes%d" % s, align_bytes=64)
+            scales = keep.tile([P, PASSES * P], U8, name="w1_scales%d" % s, align_bytes=64)
             nc.vector.quantize_mx(
                 out=codes[:].bitcast(FP8X4), scales=scales[:], in_=grouped[:].rearrange("p a c j -> p (a c j)")
             )
@@ -179,7 +176,9 @@ def tile_list_comet_page_triage_kernel(
                 )
             return acc
 
-        def write_slice(s):
+        h_of = {}
+
+        def max_of_w3_w2(s):
             cols = slice(s * P, (s + 1) * P)
             d3 = product(
                 [w3_sb[s][:, a, :].bitcast(FP8X4) for a in range(PASSES)],
@@ -191,15 +190,22 @@ def tile_list_comet_page_triage_kernel(
                 [w2_sb[s][:, a, :].bitcast(FP4X4) for a in range(PASSES)],
                 [w2_sc[:, a, cols] for a in range(PASSES)], v_w, v_sc,
             )
+            if s == SLICES - 1:
+                h_of[s] = keep.tile([P, S], F32, name="h_last", tag="h_then_codes", align_bytes=64)
+            else:
+                h_of[s] = ring2.tile([P, S], F32, name="h")
+            nc.vector.tensor_tensor(h_of[s][:], d2[:], d3_sb[:], MAX)
+
+        def max_with_w1(s):
             codes, scales = w1_q[s]
             d1 = product(
                 [codes[:, a * P : (a + 1) * P].bitcast(FP8X4) for a in range(PASSES)],
                 [scales[:, a * P : (a + 1) * P] for a in range(PASSES)], v_w, v_sc,
             )
-            h = ring2.tile([P, S], F32)
-            nc.vector.tensor_tensor(h[:], d2[:], d3_sb[:], MAX)
-            nc.vector.tensor_tensor(h[:], d1[:], h[:], MAX)
-            nc.vector.tensor_tensor(page[s][:].indirect(offs3_sb[:]), h[:], wgs_sb[:], MULT)
+            nc.vector.tensor_tensor(h_of[s][:], d1[:], h_of[s][:], MAX)
+
+        def scatter(s):
+            nc.vector.tensor_tensor(page[s][:].indirect(offs3_sb[:]), h_of[s][:], wgs_sb[:], MULT)
 
         def weigh(b_t, nt, bank_cols, p0, p1):
             nc.scalar.activation(
@@ -256,31 +262,30 @@ def tile_list_comet_page_triage_kernel(
                     weigh(b_t1[4 * half + i], 4 * half + i, bank[:, i * P : (i + 1) * P], p0, p0 + 32)
 
         quantise_w1(0)
+        max_of_w3_w2(0)
         quantise_w1(1)
         for s in range(SLICES):
-            write_slice(s)
+            max_with_w1(s)
+            if s + 1 < SLICES:
+                max_of_w3_w2(s + 1)
+            scatter(s)
             if s + 2 < SLICES:
                 quantise_w1(s + 2)
-            if s == 1:
-                turn_vectors()
-            if s in (4, 5):
-                first_pass_pair(2 * (s - 4))
-                first_pass_pair(2 * (s - 4) + 1)
-            if s == 6:
-                for nt in range(N_TILES):
-                    turn_and_weigh(b_t1[nt], nt, 4, 6)
+        turn_vectors()
+        for pair in range(4):
+            first_pass_pair(pair)
+        for nt in range(N_TILES):
+            turn_and_weigh(b_t1[nt], nt, 4, 6)
         turn_one_slice(6)
 
         v2_sc = keep.tile([P, S2], U8, tag="picked_sc0", align_bytes=64)
         nc.vector.tensor_copy(v2_sc[:], tab2_sc[:].indirect(offs2_sb[:]))
-        v2_w = []
-        for a in range(PASSES):
-            g = keep.tile([P, S2], U32, name="v2_w%d" % a, tag="picked_w%d" % a, align_bytes=64)
-            nc.vector.tensor_copy(g[:], tab2_w[a][:].indirect(offs2_sb[:]))
-            v2_w.append(g)
+        v2_w = keep.tile([P, PASSES, S2], U32, tag="wgs_then_v2", align_bytes=64)
+        for a in (1, 0):
+            nc.vector.tensor_copy(v2_w[:, a, :], tab2_w[a][:].indirect(offs2_sb[:]))
 
-        codes0 = keep.tile([P, T2], U32, align_bytes=64)
-        scales0 = keep.tile([P, T2], U8, tag="late_scales", align_bytes=64)
+        codes0 = keep.tile([P, T2], U32, tag="h_then_codes", align_bytes=64)
+        scales0 = keep.tile([P, T2], U8, align_bytes=64)
         nc.vector.quantize_mx(
             out=codes0[:].bitcast(FP8X4), scales=scales0[:], in_=woven0[:].rearrange("p h c -> p (h c)")
         )
@@ -295,24 +300,41 @@ def tile_list_comet_page_triage_kernel(
                 turn_back(b_t1[4 * half + 2 * j : 4 * half + 2 * j + 2], woven[:], j)
             quantise_b(woven, 1, half)
 
-        for m in range(M_TILES):
+        e_of, first_of, second_of = {}, {}, {}
+
+        def scores(m):
             cols = slice(m * P, (m + 1) * P)
-            e = ring3.tile([P, T2], F32)
+            e_of[m] = ring3.tile([P, T2], F32, name="e")
             for half in range(2):
                 acc = product(
-                    [v2_w[a][:, cols].bitcast(FP8X4) for a in range(PASSES)],
-                    [v2_sc[4 * a : P, cols] for a in range(PASSES)],
-                    [b_codes[a, half] for a in range(PASSES)],
-                    [b_scales[a, half] for a in range(PASSES)],
+                    [v2_w[:, a, cols].bitcast(FP8X4) for a in (1, 0)],
+                    [v2_sc[4 * a : P, cols] for a in (1, 0)],
+                    [b_codes[a, half] for a in (1, 0)],
+                    [b_scales[a, half] for a in (1, 0)],
                 )
-                nc.scalar.copy(e[:, half * BANK : (half + 1) * BANK], acc[:])
-            second = ring2.tile([P, S], F32)
-            nc.vector.tensor_copy(second[:], e[:].indirect(pos2_sb[:]))
-            first = ring2.tile([P, S], F32)
-            nc.vector.tensor_copy(first[:], e[:].indirect(pos1_sb[:]))
-            nc.vector.tensor_tensor(second[:], second[:], base_sb[:, m, :], MAX)
+                nc.scalar.copy(e_of[m][:, half * BANK : (half + 1) * BANK], acc[:])
+
+        def pick_second(m):
+            second_of[m] = ring2.tile([P, S], F32, name="second")
+            nc.vector.tensor_copy(second_of[m][:], e_of[m][:].indirect(pos2_sb[:]))
+
+        def pick_first_and_clamp(m):
+            first_of[m] = ring2.tile([P, S], F32, name="first")
+            nc.vector.tensor_copy(first_of[m][:], e_of[m][:].indirect(pos1_sb[:]))
+            nc.vector.tensor_tensor(second_of[m][:], second_of[m][:], base_sb[:, m, :], MAX)
+
+        def join(m):
             res = ring2.tile([P, S], F32)
             nc.vector.scalar_tensor_tensor(
-                res[:], first[:], vec_cols[:, N_TILES + m : N_TILES + m + 1], second[:], ADD, MULT
+                res[:], first_of[m][:], vec_cols[:, N_TILES + m : N_TILES + m + 1], second_of[m][:], ADD, MULT
             )
-            nc.sync.dma_start(out[cols, :], res[:])
+            nc.sync.dma_start(out[m * P : (m + 1) * P, :], res[:])
+
+        scores(0)
+        pick_second(0)
+        for m in range(M_TILES):
+            pick_first_and_clamp(m)
+            if m + 1 < M_TILES:
+                scores(m + 1)
+                pick_second(m + 1)
+            join(m)

@@ -18,6 +18,7 @@ MULT = mybir.AluOpType.mult
 ADD = mybir.AluOpType.add
 MAX = mybir.AluOpType.max
 COPY = mybir.ActivationFunctionType.Copy
+IDENTITY = mybir.ActivationFunctionType.Identity
 
 P = 128
 PASSES = 2
@@ -94,11 +95,12 @@ def tile_list_comet_page_triage_kernel(
         nc.vector.memset(tab_sc[:].bitcast(I32), 0)
         nc.vector.memset(w2_sc[:].bitcast(I32), 0)
         nc.vector.memset(w3_sc[:].bitcast(I32), 0)
-        nc.gpsimd.memset(tab2_sc[:].bitcast(I32), 0)
+        nc.vector.memset(tab2_sc[:].bitcast(I32), 0)
         vec_rows = keep.tile([P, P], F32)
-        nc.gpsimd.memset(vec_rows[:], 0.0)
+        nc.vector.memset(vec_rows[:], 0.0)
         ident = keep.tile([P, P], F32)
-        make_identity(nc, ident[:])
+        nc.vector.memset(ident[:], 0.0)
+        make_identity(nc, ident[:], nomemset=True)
 
         offs_sb = load_list("offs_sb", offs)
         tab_w = [load_table_words("tab_w0", tab_words, 0)]
@@ -315,19 +317,22 @@ def tile_list_comet_page_triage_kernel(
                 nc.scalar.copy(e_of[m][:, half * BANK : (half + 1) * BANK], acc[:])
 
         def pick_second(m):
-            second_of[m] = ring2.tile([P, S], F32, name="second")
+            second_of[m] = ring3.tile([P, S], F32, name="second")
             nc.vector.tensor_copy(second_of[m][:], e_of[m][:].indirect(pos2_sb[:]))
 
         def pick_first_and_clamp(m):
-            first_of[m] = ring2.tile([P, S], F32, name="first")
+            first_of[m] = ring3.tile([P, S], F32, name="first")
             nc.vector.tensor_copy(first_of[m][:], e_of[m][:].indirect(pos1_sb[:]))
             nc.vector.tensor_tensor(second_of[m][:], second_of[m][:], base_sb[:, m, :], MAX)
 
         def join(m):
             res = ring2.tile([P, S], F32)
-            nc.vector.scalar_tensor_tensor(
-                res[:], first_of[m][:], vec_cols[:, N_TILES + m : N_TILES + m + 1], second_of[m][:], ADD, MULT
-            )
+            path_col = vec_cols[:, N_TILES + m : N_TILES + m + 1]
+            if m + 1 < M_TILES:
+                nc.scalar.activation(first_of[m][:], first_of[m][:], IDENTITY, bias=path_col)
+                nc.gpsimd.tensor_tensor(res[:], first_of[m][:], second_of[m][:], MULT)
+            else:
+                nc.vector.scalar_tensor_tensor(res[:], first_of[m][:], path_col, second_of[m][:], ADD, MULT)
             nc.sync.dma_start(out[m * P : (m + 1) * P, :], res[:])
 
         scores(0)

@@ -95,12 +95,11 @@ def tile_list_comet_page_triage_kernel(
         nc.vector.memset(tab_sc[:].bitcast(I32), 0)
         nc.vector.memset(w2_sc[:].bitcast(I32), 0)
         nc.vector.memset(w3_sc[:].bitcast(I32), 0)
-        nc.vector.memset(tab2_sc[:].bitcast(I32), 0)
+        nc.gpsimd.memset(tab2_sc[:].bitcast(I32), 0)
         vec_rows = keep.tile([P, P], F32)
-        nc.vector.memset(vec_rows[:], 0.0)
+        nc.gpsimd.memset(vec_rows[:], 0.0)
         ident = keep.tile([P, P], F32)
-        nc.vector.memset(ident[:], 0.0)
-        make_identity(nc, ident[:], nomemset=True)
+        make_identity(nc, ident[:])
 
         offs_sb = load_list("offs_sb", offs)
         tab_w = [load_table_words("tab_w0", tab_words, 0)]
@@ -154,13 +153,12 @@ def tile_list_comet_page_triage_kernel(
 
         def quantise_w1(s):
             grouped = ring3.tile([P, PASSES, P, 4], BF16, align_bytes=64)
-            dst = grouped[:].rearrange("p a (c i) j -> p a c j i", i=4)
-            src = w1_raw[s].rearrange("p a j (c i) -> p a c j i", i=4)
+            src = w1_raw[s].rearrange("p a j c -> p a c j")
             if s == 0:
                 for a in range(PASSES):
-                    nc.scalar.copy(dst[:, a], src[:, a])
+                    nc.scalar.copy(grouped[:, a], src[:, a])
             else:
-                nc.scalar.copy(dst, src)
+                nc.scalar.copy(grouped[:], src)
             codes = keep.tile([P, PASSES * P], U32, name="w1_codes%d" % s, align_bytes=64)
             scales = keep.tile([P, PASSES * P], U8, name="w1_scales%d" % s, align_bytes=64)
             nc.vector.quantize_mx(
@@ -331,9 +329,12 @@ def tile_list_comet_page_triage_kernel(
             if m + 1 < M_TILES:
                 nc.scalar.activation(first_of[m][:], first_of[m][:], IDENTITY, bias=path_col)
                 nc.gpsimd.tensor_tensor(res[:], first_of[m][:], second_of[m][:], MULT)
+                nc.sync.dma_start(out[m * P : (m + 1) * P, :], res[:])
             else:
-                nc.vector.scalar_tensor_tensor(res[:], first_of[m][:], path_col, second_of[m][:], ADD, MULT)
-            nc.sync.dma_start(out[m * P : (m + 1) * P, :], res[:])
+                for j0 in (0, S // 2):
+                    js = slice(j0, j0 + S // 2)
+                    nc.vector.scalar_tensor_tensor(res[:, js], first_of[m][:, js], path_col, second_of[m][:, js], ADD, MULT)
+                    nc.sync.dma_start(out[m * P : (m + 1) * P, js], res[:, js])
 
         scores(0)
         pick_second(0)

from contextlib import ExitStack

import concourse.mybir as mybir
from concourse.masks import make_identity

K, T, H, S, T2, S2 = 1024, 2048, 1024, 512, 1024, 512
FLOPS = 3 * 2 * K * H * S + 2 * H * S2 * T2

F32 = mybir.dt.float32
BF16 = mybir.dt.bfloat16
I32 = mybir.dt.int32
U32 = mybir.dt.uint32
U16 = mybir.dt.uint16
U8 = mybir.dt.uint8
FP8X4 = mybir.dt.float8_e4m3fn_x4
FP4X4 = mybir.dt.float4_e2m1fn_x4
MULT = mybir.AluOpType.mult
ADD = mybir.AluOpType.add
MAX = mybir.AluOpType.max
COPY = mybir.ActivationFunctionType.Copy
IDENTITY = mybir.ActivationFunctionType.Identity

P = 128
PASSES = 2
BANK = 512
SLICES = H // P
N_TILES = T2 // P
M_TILES = S2 // P
W1_CHUNKS = ((0, 1), (1, 2), (2, 4), (4, 6), (6, 8))
WQ_CHUNKS = ((0, 2), (2, 5), (5, 8))


def tile_list_comet_page_triage_kernel(
    tc, tab_words, tab_scales, tab2_words, tab2_scales, w1, w2_words, w2_scales, w3_words, w3_scales,
    page0, wgs, see, path, base, offs, offs2, offs3, pos1, pos2, out,
):
    nc = tc.nc
    with ExitStack() as ctx:
        keep = ctx.enter_context(tc.tile_pool(name="keep", bufs=1))
        ring2 = ctx.enter_context(tc.tile_pool(name="ring2", bufs=2))
        ring3 = ctx.enter_context(tc.tile_pool(name="ring3", bufs=3))
        psum_mx = ctx.enter_context(tc.psum_pool(name="psum_mx", bufs=4))
        psum_t = ctx.enter_context(tc.psum_pool(name="psum_t", bufs=2))

        def load_list(name, src):
            t = keep.tile([P, S // 16], U16, name=name)
            nc.sync.dma_start(t[:], src)
            return t

        def load_table_words(name, words, a):
            t = keep.tile([P, T], U32, name=name)
            nc.sync.dma_start(t[:].bitcast(I32), words[a].rearrange("p t i -> p (t i)").bitcast(I32))
            return t

        def load_scales_side_by_side(queue, t, scales):
            for q in range(4):
                queue.dma_start(
                    t[32 * q : 32 * q + 4].bitcast(I32),
                    scales[:, 4 * q : 4 * q + 4, :].rearrange("a r c -> r a c").bitcast(I32),
                )

        def load_scales_stacked(queue, t, scales):
            for q in range(4):
                queue.dma_start(t[32 * q : 32 * q + 8].bitcast(I32), scales[:, 4 * q : 4 * q + 4, :].bitcast(I32))

        w1_raw, w2_sb, w3_sb, page = {}, {}, {}, {}

        def load_w1(s0, s1):
            t = keep.tile([P, PASSES, 4, (s1 - s0) * P], F32, name="w1_raw%d" % s0)
            for a in range(PASSES):
                rows = w1[BANK * a : BANK * (a + 1), s0 * P : s1 * P]
                nc.sync.dma_start(t[:, a], rows.rearrange("(p j) c -> p j c", j=4))
            for s in range(s0, s1):
                w1_raw[s] = t[:, :, :, (s - s0) * P : (s - s0 + 1) * P]

        def load_wq(s0, s1):
            t3 = keep.tile([P, PASSES, (s1 - s0) * P], U32, name="w3_sb%d" % s0, align_bytes=64)
            src3 = w3_words.rearrange("a p c i -> p a (c i)")[:, :, 4 * P * s0 : 4 * P * s1]
            nc.sync.dma_start(t3[:].bitcast(I32), src3.bitcast(I32))
            t2 = keep.tile([P, PASSES, (s1 - s0) * 2 * P], U8, name="w2_sb%d" % s0, align_bytes=64)
            src2 = w2_words.rearrange("a p b -> p a b")[:, :, 2 * P * s0 : 2 * P * s1]
            nc.sync.dma_start(t2[:].bitcast(I32), src2.bitcast(I32))
            for s in range(s0, s1):
                w3_sb[s] = t3[:, :, (s - s0) * P : (s - s0 + 1) * P]
                w2_sb[s] = t2[:, :, (s - s0) * 2 * P : (s - s0 + 1) * 2 * P]

        def load_page(s):
            page[s] = keep.tile([P, T2], F32, name="page%d" % s)
            nc.sync.dma_start(page[s][:], page0[s * P : (s + 1) * P, :])

        tab_sc = keep.tile([P, PASSES, T], U8)
        w3_sc = keep.tile([P, H], U8, align_bytes=64)
        w2_sc = keep.tile([P, PASSES, H], U8, align_bytes=64)
        tab2_sc = keep.tile([P, T], U8)
        nc.vector.memset(tab_sc[:].bitcast(I32), 0)
        nc.vector.memset(w2_sc[:].bitcast(I32), 0)
        nc.vector.memset(w3_sc[:].bitcast(I32), 0)
        nc.gpsimd.memset(tab2_sc[:].bitcast(I32), 0)
        vec_rows = keep.tile([P, P], F32)
        nc.gpsimd.memset(vec_rows[:], 0.0)
        ident = keep.tile([P, P], F32)
        make_identity(nc, ident[:])

        offs_sb = load_list("offs_sb", offs)
        tab_w = [load_table_words("tab_w0", tab_words, 0)]
        load_scales_side_by_side(nc.sync, tab_sc, tab_scales)
        load_wq(*WQ_CHUNKS[0])
        tab_w.append(load_table_words("tab_w1", tab_words, 1))
        load_scales_side_by_side(nc.gpsimd, w2_sc, w2_scales)
        load_scales_stacked(nc.sync, w3_sc, w3_scales)
        load_w1(*W1_CHUNKS[0])
        wgs_sb = keep.tile([P, S], F32, tag="wgs_then_v2", align_bytes=64)
        nc.sync.dma_start(wgs_sb[:], wgs)
        load_w1(*W1_CHUNKS[1])
        load_page(0)
        offs3_sb = load_list("offs3_sb", offs3)
        load_w1(*W1_CHUNKS[2])
        load_wq(*WQ_CHUNKS[1])
        load_page(1)
        load_w1(*W1_CHUNKS[3])
        load_page(2)
        nc.sync.dma_start(vec_rows[0:N_TILES, :], see.rearrange("(t p) -> t p", p=P))
        nc.sync.dma_start(vec_rows[N_TILES : N_TILES + M_TILES, :], path.rearrange("(t p) -> t p", p=P))
        load_w1(*W1_CHUNKS[4])
        load_page(3)
        load_wq(*WQ_CHUNKS[2])
        for s in range(4, SLICES):
            load_page(s)
        offs2_sb = load_list("offs2_sb", offs2)
        load_scales_stacked(nc.sync, tab2_sc, tab2_scales)
        tab2_w = [load_table_words("tab2_w%d" % a, tab2_words, a) for a in range(PASSES)]
        pos1_sb = load_list("pos1_sb", pos1)
        pos2_sb = load_list("pos2_sb", pos2)
        base_sb = keep.tile([P, M_TILES, S], F32)
        nc.sync.dma_start(base_sb[:], base.rearrange("(t p) j -> p t j", p=P))

        v_sc, v_w = [], []
        for a in range(PASSES):
            g = keep.tile([P, S], U32, name="v_w%d" % a, align_bytes=64)
            nc.vector.tensor_copy(g[:], tab_w[a][:].indirect(offs_sb[:]))
            v_w.append(g)
            g = keep.tile([P, S], U8, name="v_sc%d" % a, tag="picked_sc%d" % a, align_bytes=64)
            nc.vector.tensor_copy(g[:], tab_sc[:, a, :].indirect(offs_sb[:]))
            v_sc.append(g)

        w1_q = {}
        vec_cols = keep.tile([P, N_TILES + M_TILES], F32)

        def turn_vectors():
            vec_ps = psum_t.tile([P, BANK], F32, tag="back")
            nc.tensor.transpose(vec_ps[:, 0:P], vec_rows[:], ident[:])
            nc.scalar.copy(vec_cols[:], vec_ps[:, 0 : N_TILES + M_TILES])

        def quantise_w1(s):
            grouped = ring3.tile([P, PASSES, P, 4], BF16, align_bytes=64)
            src = w1_raw[s].rearrange("p a j c -> p a c j")
            if s == 0:
                for a in range(PASSES):
                    nc.scalar.copy(grouped[:, a], src[:, a])
            else:
                nc.scalar.copy(grouped[:], src)
            codes = keep.tile([P, PASSES * P], U32, name="w1_codes%d" % s, align_bytes=64)
            scales = keep.tile([P, PASSES * P], U8, name="w1_scales%d" % s, align_bytes=64)
            nc.vector.quantize_mx(
                out=codes[:].bitcast(FP8X4), scales=scales[:], in_=grouped[:].rearrange("p a c j -> p (a c j)")
            )
            w1_q[s] = (codes, scales)

        def product(lhs_codes, lhs_scales, rhs_codes, rhs_scales):
            acc = psum_mx.tile([P, BANK], F32, name="acc")
            for a in range(PASSES):
                nc.tensor.matmul_mx(
                    out=acc[:], lhsT=lhs_codes[a], lhsT_scale=lhs_scales[a],
                    rhs=rhs_codes[a][:].bitcast(FP8X4), rhs_scale=rhs_scales[a][:],
                    start=(a == 0), stop=(a == PASSES - 1),
                )
            return acc

        h_of = {}

        def max_of_w3_w2(s):
            cols = slice(s * P, (s + 1) * P)
            d3 = product(
                [w3_sb[s][:, a, :].bitcast(FP8X4) for a in range(PASSES)],
                [w3_sc[4 * a : P, cols] for a in range(PASSES)], v_w, v_sc,
            )
            d3_sb = ring2.tile([P, S], F32)
            nc.scalar.copy(d3_sb[:], d3[:])
            d2 = product(
                [w2_sb[s][:, a, :].bitcast(FP4X4) for a in range(PASSES)],
                [w2_sc[:, a, cols] for a in range(PASSES)], v_w, v_sc,
            )
            if s == SLICES - 1:
                h_of[s] = keep.tile([P, S], F32, name="h_last", tag="h_then_codes", align_bytes=64)
            else:
                h_of[s] = ring2.tile([P, S], F32, name="h")
            nc.vector.tensor_tensor(h_of[s][:], d2[:], d3_sb[:], MAX)

        def max_with_w1(s):
            codes, scales = w1_q[s]
            d1 = product(
                [codes[:, a * P : (a + 1) * P].bitcast(FP8X4) for a in range(PASSES)],
                [scales[:, a * P : (a + 1) * P] for a in range(PASSES)], v_w, v_sc,
            )
            nc.vector.tensor_tensor(h_of[s][:], d1[:], h_of[s][:], MAX)

        def scatter(s):
            nc.vector.tensor_tensor(page[s][:].indirect(offs3_sb[:]), h_of[s][:], wgs_sb[:], MULT)

        def weigh(b_t, nt, bank_cols, p0, p1):
            nc.scalar.activation(
                b_t[:, :, p0:p1, :], bank_cols.rearrange("n (p u e) -> n u p e", u=2, e=2), COPY,
                scale=vec_cols[:, nt : nt + 1],
            )

        def turn_and_weigh(b_t, nt, s0, s1):
            bank = psum_t.tile([P, BANK], F32, tag="turn")
            for s in range(s0, s1):
                nc.tensor.transpose(
                    bank[:, (s - s0) * P : (s - s0 + 1) * P], page[s][:, nt * P : (nt + 1) * P], ident[:]
                )
            weigh(b_t, nt, bank[:, 0 : (s1 - s0) * P], 32 * (s0 % 4), 32 * (s0 % 4) + 32 * (s1 - s0))

        def turn_back(b_pair, woven, j):
            bank = psum_t.tile([P, 2, 2, P], F32, tag="back")
            for i in range(2):
                words = b_pair[i][:].rearrange("n u p e -> n (u p e)").bitcast(F32)
                for u in range(2):
                    nc.tensor.transpose(bank[:, i, u, :], words[:, u * P : (u + 1) * P], ident[:])
            dst = woven.bitcast(F32).rearrange("p (i n u) -> p i n u", i=4, u=2)[:, 2 * j : 2 * j + 2]
            nc.scalar.copy(dst, bank[:].rearrange("p i u n -> p i n u"))

        b_codes = {}
        b_scales = {}

        def quantise_b(woven, a, half):
            b_codes[a, half] = keep.tile([P, BANK], U32, name="b_codes%d%d" % (a, half), align_bytes=64)
            b_scales[a, half] = keep.tile([P, BANK], U8, name="b_scales%d%d" % (a, half), align_bytes=64)
            nc.vector.quantize_mx(out=b_codes[a, half][:].bitcast(FP8X4), scales=b_scales[a, half][:], in_=woven[:])

        woven0 = keep.tile([P, 2, 4 * BANK], BF16, align_bytes=64)

        def first_pass_pair(pair):
            half, j = divmod(pair, 2)
            b_pair = []
            for i in range(2):
                b_t = ring3.tile([P, 2, P, 2], BF16, name="b_t0")
                turn_and_weigh(b_t, 2 * pair + i, 0, 4)
                b_pair.append(b_t)
            turn_back(b_pair, woven0[:, half, :], j)

        b_t1 = [keep.tile([P, 2, P, 2], BF16, name="b_t1_%d" % nt) for nt in range(N_TILES)]

        def turn_one_slice(s):
            for half in range(2):
                bank = psum_t.tile([P, BANK], F32, tag="turn")
                for i in range(4):
                    nt = 4 * half + i
                    nc.tensor.transpose(bank[:, i * P : (i + 1) * P], page[s][:, nt * P : (nt + 1) * P], ident[:])
                for i in range(4):
                    p0 = 32 * (s % 4)
                    weigh(b_t1[4 * half + i], 4 * half + i, bank[:, i * P : (i + 1) * P], p0, p0 + 32)

        quantise_w1(0)
        max_of_w3_w2(0)
        quantise_w1(1)
        for s in range(SLICES):
            max_with_w1(s)
            if s + 1 < SLICES:
                max_of_w3_w2(s + 1)
            scatter(s)
            if s + 2 < SLICES:
                quantise_w1(s + 2)
        turn_vectors()
        for pair in range(4):
            first_pass_pair(pair)
        for nt in range(N_TILES):
            turn_and_weigh(b_t1[nt], nt, 4, 6)
        turn_one_slice(6)

        v2_sc = keep.tile([P, S2], U8, tag="picked_sc0", align_bytes=64)
        nc.vector.tensor_copy(v2_sc[:], tab2_sc[:].indirect(offs2_sb[:]))
        v2_w = keep.tile([P, PASSES, S2], U32, tag="wgs_then_v2", align_bytes=64)
        for a in (1, 0):
            nc.vector.tensor_copy(v2_w[:, a, :], tab2_w[a][:].indirect(offs2_sb[:]))

        codes0 = keep.tile([P, T2], U32, tag="h_then_codes", align_bytes=64)
        scales0 = keep.tile([P, T2], U8, align_bytes=64)
        nc.vector.quantize_mx(
            out=codes0[:].bitcast(FP8X4), scales=scales0[:], in_=woven0[:].rearrange("p h c -> p (h c)")
        )
        for half in range(2):
            b_codes[0, half] = codes0[:, half * BANK : (half + 1) * BANK]
            b_scales[0, half] = scales0[:, half * BANK : (half + 1) * BANK]

        turn_one_slice(7)
        for half in range(2):
            woven = ring2.tile([P, 4 * BANK], BF16, name="woven", align_bytes=64)
            for j in range(2):
                turn_back(b_t1[4 * half + 2 * j : 4 * half + 2 * j + 2], woven[:], j)
            quantise_b(woven, 1, half)

        e_of, first_of, second_of = {}, {}, {}

        def scores(m):
            cols = slice(m * P, (m + 1) * P)
            e_of[m] = ring3.tile([P, T2], F32, name="e")
            for half in range(2):
                acc = product(
                    [v2_w[:, a, cols].bitcast(FP8X4) for a in (1, 0)],
                    [v2_sc[4 * a : P, cols] for a in (1, 0)],
                    [b_codes[a, half] for a in (1, 0)],
                    [b_scales[a, half] for a in (1, 0)],
                )
                nc.scalar.copy(e_of[m][:, half * BANK : (half + 1) * BANK], acc[:])

        def pick_second(m):
            second_of[m] = ring3.tile([P, S], F32, name="second")
            nc.vector.tensor_copy(second_of[m][:], e_of[m][:].indirect(pos2_sb[:]))

        def pick_first_and_clamp(m):
            first_of[m] = ring3.tile([P, S], F32, name="first")
            nc.vector.tensor_copy(first_of[m][:], e_of[m][:].indirect(pos1_sb[:]))
            nc.vector.tensor_tensor(second_of[m][:], second_of[m][:], base_sb[:, m, :], MAX)

        def join(m):
            res = ring2.tile([P, S], F32)
            path_col = vec_cols[:, N_TILES + m : N_TILES + m + 1]
            if m + 1 < M_TILES:
                nc.scalar.activation(first_of[m][:], first_of[m][:], IDENTITY, bias=path_col)
                nc.gpsimd.tensor_tensor(res[:], first_of[m][:], second_of[m][:], MULT)
                nc.sync.dma_start(out[m * P : (m + 1) * P, :], res[:])
            else:
                for j0 in (0, S // 2):
                    js = slice(j0, j0 + S // 2)
                    nc.vector.scalar_tensor_tensor(res[:, js], first_of[m][:, js], path_col, second_of[m][:, js], ADD, MULT)
                    nc.sync.dma_start(out[m * P : (m + 1) * P, js], res[:, js])

        scores(0)
        pick_second(0)
        for m in range(M_TILES):
            pick_first_and_clamp(m)
            if m + 1 < M_TILES:
                scores(m + 1)
                pick_second(m + 1)
            join(m)
